import numpy as np, ml_dtypes
CORES = [24,25,26,27,28,29,30,31]
N = 8
import mx_ref
BF = ml_dtypes.bfloat16
def entries(a):
    return np.ascontiguousarray(a.T).reshape(-1)
def table(e):
    return np.ascontiguousarray(np.reshape(e, (-1, 16)).T).astype(np.int32)
def cols(t, e):
    v = np.concatenate([t.reshape(128, -1, 4), np.zeros((128, 1, 4), BF)], axis=1)
    return np.ascontiguousarray(v[:, e]).reshape(128, -1)
def tile(rs):
    return np.stack(rs, axis=2).reshape(128, -1).astype(BF)
def cut(t, i, w=512):
    return t[:, w * i:w * i + w]
def f(rng, *shape):
    return mx_ref.flush((rng.standard_normal(shape, dtype=np.float32) * np.exp2(rng.integers(-2, 3, shape[:-1] + (1,)))).astype(BF))
def wide(rng, *shape, cols=0):
    v = rng.standard_normal(shape, dtype=np.float32) * np.exp2(rng.integers(-12, 13, shape)).astype(np.float32)
    if cols: v *= np.repeat(np.exp2(rng.integers(-cols, cols + 1, shape[:-2] + (1, shape[-1] // 4))) * (rng.random(shape[:-2] + (1, shape[-1] // 4)) > 0.0625), 4, axis=-1).astype(np.float32)
    return mx_ref.flush(v.astype(BF))
S, C1, C2 = 256, 24, 40
def pack(nb):
    return {"nb0": np.stack([table(e) for e in nb[0].reshape(N, S)]), "nb1": np.stack([table(e) for e in nb[1].reshape(N, S)])}
def lists(rng):
    pool = [[(q * S + rng.permutation(S)[:rng.integers(1, 3 * C1 // 4 + 1)]).tolist() for q in range(N)] for r in range(N)]
    skew = []
    for r in range(N):
        p = np.exp2(rng.integers(0, 4, N)).astype(float); p[r] = 0
        skew.append(np.divide(p, p.sum()))
    who = {n: [] for n in range(N * S)}
    near, hand = {}, {}
    for r in range(N):
        for q in range(N):
            if q == r: continue
            for n in pool[r][q]: who[n].append(r)
            near[r, q] = set(pool[r][q]); hand[r, q] = set(pool[r][q])
    def one(r):
        if rng.random() < 0.6: return int(r * S + rng.integers(0, S))
        p = pool[r][int(rng.choice(N, p=skew[r]))]
        return p[rng.integers(0, len(p))]
    def fits(n, w):
        return all((w // S == r or len(near[r, w // S] | {w}) <= C2) and len(hand[r, n // S] | {w}) <= C2 for r in who[n])
    nb = np.zeros((2, N * S), int)
    for n in rng.permutation(N * S).tolist():
        for k in range(2):
            for _ in range(8):
                w = one(n // S)
                if fits(n, w): break
            else: w = n
            nb[k, n] = w
            for r in who[n]:
                if w // S != r: near[r, w // S].add(w)
                hand[r, n // S].add(w)
    for r in range(N):
        free = rng.permutation([n for n in range(r * S, r * S + S) if not who[n]])
        nb[1, free[:S // 20]] = nb[0, free[:S // 20]]
        for k in range(2):
            p = rng.permutation(free)[:2 * (S >> 6)]
            nb[k, p] = p[::-1]
    return pack(nb)
def weights(rng, n):
    return np.stack([f(rng, 128, 512 * n)] * N)
def setup_inputs(rng):
    return {"x": f(rng, N, 128, 4 * S), "a": weights(rng, 8), "v": weights(rng, 2), "u": weights(rng, 2), **lists(rng)}
def setup_inputs_apart(rng):
    d = setup_inputs(rng)
    nb = np.zeros((2, N * S), int)
    e, m = C2 - C1, S - (N - 1) * C1
    h = min(-(-m // (N - 1)), e - 2)
    p = [q * S + rng.permutation(S) for q in range(N)]
    F, H = {}, {}
    for q in range(N):
        for i in range(N - 1):
            r = (q + 1 + i) % N
            F[r, q] = p[q][C1 * i:C1 * i + C1]
            H[r, q] = p[q][(N - 1) * C1 + (h * i + np.arange(h)) % m]
    for r, q in F:
        s = (q + 1) % N
        if s == r: s = (q + 2) % N
        D = np.concatenate([H[r, q], rng.permutation(F[q, s])[:e - h]])
        k = (r + q) % 2
        nb[k, F[r, q]] = rng.permutation(F[q, r])
        nb[1 - k, F[r, q]] = np.concatenate([rng.permutation(D), F[q, r][:C1 - e]])
    for r in range(N):
        rest = p[r][(N - 1) * C1:]
        far = np.concatenate([F[r, q] for q in range(N) if q != r])
        for k in range(2):
            must = [int(n) for q in range(N) if q != r and (r + q) % 2 != k for n in F[r, q][C1 - e:e]]
            nb[k, rest] = rng.permutation(must + rng.choice(np.concatenate([far, p[r]]), m - len(must)).tolist())
    return {**d, **pack(nb)}
def setup_inputs_full(rng):
    d = setup_inputs(rng)
    nb = np.zeros((2, N * S), int)
    p = [q * S + rng.permutation(S) for q in range(N)]
    B = [e[:C1] for e in p]
    for q in range(N):
        some = rng.permutation(np.concatenate(B))[:C1]
        nb[:, B[q]] = rng.permutation(np.concatenate([p[q][C1:C2], some, rng.choice(some, 2 * C1 - C2)])).reshape(2, C1)
        rest = p[q][C1:]
        far = np.concatenate([B[s] for s in range(N) if s != q])
        for k in range(2):
            nb[k, rest] = rng.permutation(np.concatenate([far, rng.choice(np.concatenate([far, p[q]]), len(rest) - len(far))]))
    return {**d, **pack(nb)}
def setup_inputs_hub(rng):
    d = setup_inputs(rng)
    nb = np.zeros((2, N * S), int)
    for r in range(N):
        for k in range(2): nb[k, r * S:r * S + S] = (r + rng.integers(1, N)) % N * S + rng.integers(0, S)
    return {**d, **pack(nb)}
def setup_inputs_spread(rng):
    d = setup_inputs(rng); d["x"] = wide(rng, N, 128, 4 * S); return d
def setup_inputs_most(rng):
    d = setup_inputs(rng)
    nb = np.zeros((2, N * S), int)
    p = [q * S + rng.permutation(S) for q in range(N)]
    B = [e[:C1] for e in p]
    for q in range(N):
        nb[:, B[q]] = rng.permutation(np.concatenate([p[q][:C2], rng.choice(p[q][:C2], 2 * C1 - C2)])).reshape(2, C1)
        far = np.concatenate([B[s] for s in range(N) if s != q])
        must = np.concatenate([far, p[q][C2:]])
        nb[:, p[q][C1:]] = rng.permutation(np.concatenate([must, rng.choice(np.concatenate([far, p[q]]), 2 * (S - C1) - len(must))])).reshape(2, S - C1)
    return {**d, **pack(nb)}
def check_inputs(d):
    b = []
    nb = np.stack([np.concatenate([entries(e) for e in d[n]]) for n in ("nb0", "nb1")])
    for n in ("a", "v", "u"):
        if (d[n] != d[n][:1]).any(): b.append(n + " isn't the same on all ranks")
    if nb.min() < 0 or nb.max() >= N * S: return b + ["nb0, nb1"]
    for r in range(N):
        own = nb[:, r * S:r * S + S]
        first = np.unique(own)
        near = np.unique(np.concatenate([first, nb[0][first], nb[1][first]]))
        for q in range(N):
            if q == r: continue
            if (first // S == q).sum() > C1: b.append("too many neighbours on one other rank")
            if (near // S == q).sum() > C2: b.append("too many nodes of one other rank in two steps")
            behind = np.concatenate([nb[k][own[k][own[k] // S == q]] for k in range(2)])
            if len(np.unique(behind)) > C2: b.append("too many nodes behind neighbours on one other rank")
    return b
def product(w, t, e):
    n, i = np.unique(e, return_inverse=True)
    n = np.concatenate([n, np.full(-len(n) % 16, n[0])])
    return mx_ref.matmul(mx_ref.quantize(np.ascontiguousarray(w)), mx_ref.quantize(cols(t, n)))[:, i.reshape(-1)]
def reference(x, a, v, u, nb0, nb1):
    nb = np.stack([np.concatenate([entries(e) for e in n]) for n in (nb0, nb1)])
    x = np.concatenate(list(x), axis=1)
    named = np.unique(nb)
    R = []
    for b in range(4):
        P = product(cut(a[0], b), x, nb[0][named]) + product(cut(a[0], 4 + b), x, nb[1][named])
        R.append(np.maximum(P, np.float32(0)) * np.float32(0.05))
    h = np.zeros((128, N * S, 4), BF)
    h[:, named] = tile(R).reshape(128, -1, 4)
    h = h.reshape(128, -1)
    y = product(cut(v[0], 0), h, nb[0]) + product(cut(v[0], 1), h, nb[1]) + product(cut(u[0], 0), x, nb[0][nb[0]]) + product(cut(u[0], 1), x, nb[1][nb[1]])
    return {"y": np.stack([y[:, r * S:r * S + S] for r in range(N)])}

from concourse.bass import DstId, RemoteDMATransfer
from concourse.mybir import dt, AluOpType, AxisListType, ActivationFunctionType

N, S, C1 = 8, 256, 24
NV = 10
POOL = S + 7 * C1
UPOOL = 2 * S + 7 * 2 * C1

F32, BF, I32, U16, F16, CODE, PLANE = "float32", "bfloat16", "int32", "uint16", "float16", "float8_e4m3fn_x4", "uint8"
SCRATCH = {}


def _sb(dtype, **bufs):
    for name in bufs:
        SCRATCH[name] = ("sbuf", [128, bufs[name]], dtype)


_sb(I32, w32=16, w16=32, u1=32, u2=32, u3=32, u4=32, u5=32, u6=32, u7=32)
_sb(F16, z16=512, zh=512, row=512, cum=256 * NV + 8)
_sb(BF, rowb=512, eq=512 * NV, sj=512 * (17 - NV), fw=320, fm=32, fs=32, um=48, us=48, tb1=16, tb2=64,
    z2=2048, zh2=2048, tab=2048, gm=512, gs=512)
_sb(F32, sa=24, cntd=16, bit=16, nbit=16, pre=16, zz=16, yy=16, tot=32, tott=32, off=1, uf=3, tb0=16,
    bp=32, eu=32, ef=16, pf=32, pu=32)
_sb(U16, p16=16, sf=2, su=3, rho=32, po16=32, pu16=32, lf=14, lr=14, lu=21, lru=22)
_sb(I32, it=16, li=16, pi=1, pai=1, pmi=1, pgi=1, pci=1)
_sb(F32, bi=16, tr=16, ownc=16, oc0=16, pm=1, pg=1, own=1, nown=1, trow=32, tg=32,
    m1=32, m2=32, mm=32, one=16, addu=4)
_sb(BF, loc=16, gcol=1, pa=1, idr=256, jm=512, mk=512, hm=2048, h16=512)
_sb(BF, xb=1024, ab=4096, vb=1024, ub=1024, ht=1024)
_sb(F32, yo=S)
for _n, _w in dict(aq=1024, vq=256, uq=256, xq=S, xg=224, xp=POOL, xk=512, xu=336, up=UPOOL, yu=512, hq=S, hg=224,
                   hp=POOL, yh=512).items():
    SCRATCH[_n] = ("sbuf", [128, _w], CODE)
    SCRATCH[_n + "s"] = ("sbuf", [128, _w], PLANE)
for _n in ("ps0", "ps1", "ps2", "ps3", "psy"):
    SCRATCH[_n] = ("psum", [128, 512], F32)
SEMAPHORES = ["lw", "lw2", "lx", "la", "lv", "vs", "ss", "ts", "gc", "rt", "rf", "ru", "xo", "uc", "st", "ls",
              "af", "au", "axc", "axs", "auc", "aus", "ahc", "ahs"]


def rank_program(g, core, T, topo):
    rank = T.rank_of(core)
    if rank is None:
        return
    A, Fn = AluOpType, ActivationFunctionType
    vec, sca, syn, ten, sem = g.vector, g.scalar, g.sync, g.tensor, T.sem
    queue = {"v": vec, "s": sca, "y": syn, "t": ten, "g": g}
    cnt = {"vs": 0, "ss": 0, "ts": 0, "gc": 0}
    seen = {}

    def did(name, ins):
        ins.then_inc(sem[name], 1)
        cnt[name] += 1
        return cnt[name]

    def wait(q, name, val):
        if seen.get((q, name), 0) < val:
            seen[(q, name)] = val
            queue[q].wait_ge(sem[name], val)

    def V(ins):
        return did("vs", ins)

    def vw(n):
        wait("v", "vs", n)

    def words(ap):
        return ap.bitcast(dt.uint32)

    def copy(out, in_):
        return V(vec.tensor_copy(out, in_))

    def ts(out, in0, s1, op0, s2=None, op1=None):
        if op1 is None:
            return V(vec.tensor_scalar(out, in0, s1, None, op0))
        return V(vec.tensor_scalar(out, in0, s1, s2, op0, op1))

    def tt(out, in0, in1, op):
        return V(vec.tensor_tensor(out, in0, in1, op))

    def fill(ap, val):
        return V(vec.memset(ap, val))

    def quant(out, sc, in_):
        return V(vec.quantize_mx(out, sc, in_))

    def hold(out, keep, data):
        return V(vec.tensor_tensor_scan(out, keep, data, 0.0, A.mult, A.add))

    def act(out, in_, fn=Fn.Copy, **kw):
        return did("ss", sca.activation(out, in_, fn, **kw))

    def load(q, out, in_, name):
        queue[q].dma_start(out, in_).then_inc(sem[name], 16)

    dest = [T.cores[(rank + 1 + i) % N] for i in range(N - 1)]
    masks = [0] * (N - 1)
    near, far = 0, 0
    for i, d in enumerate(dest):
        e = topo.engines(core, d)
        if topo.die(d) != topo.die(core):
            masks[i] = (1 << e[4 * far]) | (1 << e[4 * far + 2])
            far += 1
        else:
            masks[i] = (1 << e[4 * near + 1]) | (1 << e[4 * near + 3])
            near += 1

    def send(src, dst, name):
        tr = []
        for i, d in enumerate(dest):
            rid, pid, _e = topo.addr(d)
            tr.append(RemoteDMATransfer(dst_ids=[DstId(rid=rid, pnc=pid)], dma_engine_mask=masks[i],
                                        remote_sem=sem[name], src=src(i), dst=dst(6 - i)))
        g.remote_dma_fused(tr, local_sem=sem.ls)

    ARR = 2 * (N - 1)

    for b in range(4):
        load("y", T.w32[32 * b:32 * b + 16, :], T.nb0[:], "lw")
        load("s", T.w32[32 * b + 16:32 * b + 32, :], T.nb1[:], "lw")
    load("y", T.xb[:], T.x[:], "lx")
    load("y", T.ab[:], T.a[:], "la")
    for q in range(8):
        load("y", T.w16[16 * q:16 * q + 16, 0:16], T.nb0[:], "lw2")
        load("s", T.w16[16 * q:16 * q + 16, 16:32], T.nb1[:], "lw2")

    def iota(out, pattern, mul, small=True):
        if small:
            return did("gc", g.iota(out, pattern, 0, mul, allow_small_or_imprecise_dtypes=True))
        return did("gc", g.iota(out, pattern, 0, mul))
    iota(T.pi[:], [[1, 1]], 1, False)
    g_int = iota(T.it[:], [[1, 16]], 16, False)
    iota(T.trow[:], [[1, 32]], 0)
    iota(T.tg[:], [[1, 2], [0, 16]], 0)
    g_48 = iota(T.jm[:, 0:48], [[0, 3], [1, 16]], 0)
    iota(T.idr[:], [[1, 16], [16, 16]], 0)
    g_all = iota(T.jm[:, 48:512], [[0, 29], [1, 16]], 0)

    k = fill(T.hm[:, 0:512], 1.0)
    fill(T.one[:], 1.0)
    fill(T.fw[:, 0:32], 0.0)
    vw(k)
    k_hm = fill(T.hm[:, 0:512:32], 0.0)
    k = fill(T.h16[:], 1.0)
    vw(k_hm)
    ts(T.z16[:], T.hm[:, 0:512], 0.0, A.mult)
    ts(T.cum[:, 0:8], T.hm[:, 0:8], 0.0, A.mult)
    vw(k)
    fill(T.h16[:, 0:512:16], 0.0)
    wait("v", "gc", g_int)
    ts(T.pci[:], T.pi[:], 4, A.logical_shift_right)
    k = ts(T.li[:], T.it[:], 255, A.bitwise_and)
    ts(T.pai[:], T.pi[:], 15, A.bitwise_and)
    ts(T.pmi[:], T.pi[:], 31, A.bitwise_and)
    k2 = ts(T.pgi[:], T.pi[:], 4, A.logical_shift_right, 1, A.bitwise_and)
    vw(k)
    ts(T.gcol[:], T.pci[:], -256.0, A.mult)
    copy(T.loc[:], T.li[:])
    ts(T.bi[:], T.li[:], -1.0, A.mult, -0.5, A.add)
    vw(k2)
    copy(T.pm[:], T.pmi[:])
    copy(T.pg[:], T.pgi[:])
    k = copy(T.pa[:], T.pai[:])
    ts(T.own[:], T.pci[:], float(rank), A.is_equal)
    ts(T.nown[:], T.pci[:], float(rank), A.not_equal)
    ts(T.tr[:], T.li[:], 33.0, A.add)
    wait("v", "gc", g_48)
    vw(k)
    ts(T.m1[:], T.trow[:], T.pm[:, 0:1], A.is_gt)
    k = ts(T.m2[:], T.tg[:], T.pg[:, 0:1], A.is_equal)
    ts(T.mk[:, 0:48], T.jm[:, 0:48], T.pa[:, 0:1], A.is_equal)
    vw(k)
    tt(T.mm[:], T.m1[:], T.m2[:], A.mult)

    wait("v", "lw", 128)
    k = copy(T.z16[:, 0:512:32], T.w32[:])
    vw(k)
    k = hold(T.zh[:], T.hm[:, 0:512], T.z16[:])
    vw(k)
    k = V(vec.transpose(T.row[:], T.zh[:]))
    vw(k)
    k_row = ts(T.rowb[:], T.row[:], T.gcol[:, 0:1], A.add)
    wait("s", "vs", k_row)
    for m in range(17 - NV):
        c = NV - 1 + m
        s_sum = act(T.sj[:, 512 * m:512 * m + 512], T.rowb[:], Fn.Sign, bias=T.bi[:, c:c + 1], scale=1.0,
                    accum_out=T.sa[:, m:m + 1])
    vw(k_row)
    for c in range(NV):
        k = ts(T.eq[:, 512 * c:512 * c + 512], T.rowb[:], T.loc[:, c:c + 1], A.is_equal)
    vw(k)
    k = V(vec.tensor_tensor_scan(T.cum[:, 8:8 + 256 * NV], T.eq[:, 0:512 * NV:2], T.eq[:, 1:512 * NV:2], 0.0,
                                 A.add, A.add))
    vw(k)
    tt(T.cntd[:, 0:NV], T.cum[:, 263:8 + 256 * NV:256], T.cum[:, 7:8 + 256 * (NV - 1):256], A.subtract)
    wait("v", "ss", s_sum)
    k = tt(T.cntd[:, NV:16], T.sa[:, 0:16 - NV], T.sa[:, 1:17 - NV], A.subtract)
    vw(k)
    k = ts(T.bit[:], T.cntd[:], 0.0, A.is_gt, T.nown[:, 0:1], A.mult)
    vw(k)
    k_pre = hold(T.pre[:], T.one[:], T.bit[:])
    k_nb = ts(T.nbit[:], T.bit[:], -1.0, A.mult, 1.0, A.add)
    vw(k_pre)
    k_tot = ts(T.tot[:], T.mm[:], T.pre[:, 15:16], A.mult)
    vw(k_nb)
    k_zz = tt(T.zz[:], T.nbit[:], T.tr[:], A.mult)
    vw(k_tot)
    k_tott = V(vec.transpose(T.tott[:], T.tot[:]))
    vw(k_zz)
    tt(T.yy[:], T.pre[:], T.zz[:], A.max)
    vw(k_tott)
    k_off = V(vec.tensor_reduce(T.off[:], T.tott[:], AxisListType.X, A.add))
    vw(k_off)
    k_p16 = ts(T.p16[:], T.yy[:], T.off[:, 0:1], A.add, -1.0, A.add)
    wait("v", "gc", g_all)
    vw(k_p16)
    k_sc = copy(T.fw[:, 0:320].indirect(T.p16[:, 0:16]), T.idr[:])
    vw(k_sc)
    k = tt(T.fm[:], T.fw[:, 0:32], T.mk[:, 0:32], A.mult)
    vw(k)
    k = hold(T.fs[:], T.h16[:, 0:32], T.fm[:])
    vw(k)
    k_sf = copy(T.sf[:], T.fs[:, 15:32:16])

    wait("g", "vs", k_sf)
    send(lambda i: T.sf[:], lambda j: T.lf[:, 2 * j:2 * j + 2], "af")

    ts(T.tb0[:], T.pre[:], T.off[:, 0:1], A.add, T.nown[:, 0:1], A.mult)
    k = ts(T.oc0[:], T.loc[:], -231.0, A.add, T.own[:, 0:1], A.mult)
    tt(T.um[:, 0:24], T.fw[:, 0:24], T.mk[:, 0:24], A.mult)
    k2 = tt(T.um[:, 24:48], T.fw[:, 0:24], T.mk[:, 24:48], A.mult)
    fill(T.addu[:, 0:1], 0.0)
    fill(T.addu[:, 2:3], 256.0)
    vw(k)
    k = ts(T.ownc[:], T.oc0[:], -1.0, A.add)
    vw(k2)
    k2 = hold(T.us[:], T.h16[:, 0:48], T.um[:])
    vw(k)
    k_tb = tt(T.tb1[:], T.tb0[:], T.ownc[:], A.add)
    k2 = ts(T.addu[:, 1:2], T.pa[:], 8.0, A.is_ge, 256.0, A.mult)
    wait("v", "lx", 16)
    k_xq = quant(T.xq[:], T.xqs[:], T.xb[:])
    vw(k2)
    k = tt(T.uf[:], T.us[:, 15:48:16], T.addu[:, 0:3], A.add)
    wait("v", "lw2", 256)
    ts(T.u1[:], T.w16[:], 63, A.bitwise_and)
    ts(T.u2[:], T.w16[:], 6, A.logical_shift_right)
    vw(k)
    k_su = copy(T.su[:], T.uf[:])
    wait("g", "vs", k_su)
    send(lambda i: T.su[:], lambda j: T.lu[:, 3 * j:3 * j + 3], "au")

    wait("y", "vs", k_tb)
    for b in range(4):
        load("y", T.tb2[32 * b:32 * b + 32, :], T.tb1[:], "rt")
    wait("y", "vs", k_xq)
    load("y", T.xp[:, 0:S].bitcast(dt.uint8), T.xq[:].bitcast(dt.uint8), "xo")
    load("y", T.xps[:, 0:S], T.xqs[:], "xo")
    for m in range(4):
        act(T.z2[:, 512 * m:512 * m + 512], T.hm[:, 0:512], scale=0.0)
    for m in range(1, 4):
        s_hm = act(T.hm[:, 512 * m:512 * m + 512], T.hm[:, 0:512])
    wait("y", "af", ARR)
    wait("s", "af", ARR)
    for q in range(8):
        load("ys"[q % 2], T.lr[16 * q:16 * q + 16, :], T.lf[16 * rank:16 * rank + 16, :], "rf")
    load("y", T.vb[:], T.v[:], "lv")
    load("y", T.ub[:], T.u[:], "lv")
    wait("y", "au", ARR)
    for q in range(8):
        load("y", T.lru[16 * q:16 * q + 16, 0:21], T.lu[16 * rank:16 * rank + 16, :], "ru")

    k = ts(T.u3[:], T.w16[:], 8, A.logical_shift_right)
    vw(k)
    k2 = ts(T.u4[:], T.u1[:], 32, A.mult)
    k = ts(T.u5[:], T.u3[:], 8 - rank, A.add)
    ts(T.mk[:, 48:512], T.jm[:, 48:512], T.pa[:, 0:1], A.is_equal)
    vw(k)
    k2 = tt(T.u6[:], T.u4[:], T.u2[:], A.add)
    k = ts(T.u7[:], T.u5[:], 7, A.bitwise_and)
    vw(k)
    ts(T.bp[:], T.u7[:], 24.0, A.mult, 232.0, A.add)
    ts(T.ef[:], T.u7[:, 0:16], 0.0, A.is_gt, 232.0, A.mult)
    ts(T.eu[:, 16:32], T.u7[:, 16:32], 24.0, A.mult, 256.0, A.add)
    k = ts(T.eu[:, 0:16], T.u7[:, 0:16], 24.0, A.mult)
    copy(T.rho[:], T.u6[:])
    vw(k)
    tt(T.eu[:, 0:16], T.eu[:, 0:16], T.ef[:], A.add)
    wait("v", "la", 16)
    quant(T.aq[:, 0:512], T.aqs[:, 0:512], T.ab[:, 0:2048])
    quant(T.aq[:, 512:1024], T.aqs[:, 512:1024], T.ab[:, 2048:4096])
    wait("v", "rt", 64)
    wait("v", "ss", s_hm)
    k = copy(T.z2[:, 0:2048:32], T.tb2[:])
    vw(k)
    k_zh2 = hold(T.zh2[:], T.hm[:], T.z2[:])

    wait("v", "rf", 128)
    k_xs = copy(words(T.xg[:, 0:224]), words(T.xq[:, 0:S]).indirect(T.lr[:, 0:14]))
    wait("s", "rf", 128)
    wait("s", "vs", k_xq)
    s_xs = act(T.xgs[:, 0:224], T.xqs[:, 0:S].indirect(T.lr[:, 0:14]))
    wait("g", "vs", k_xs)
    send(lambda i: T.xg[:, 32 * i:32 * i + C1].bitcast(dt.uint8),
         lambda j: T.xp[:, S + C1 * j:S + C1 * j + C1].bitcast(dt.uint8), "axc")
    wait("g", "ss", s_xs)
    send(lambda i: T.xgs[:, 32 * i:32 * i + C1], lambda j: T.xps[:, S + C1 * j:S + C1 * j + C1], "axs")

    vw(k_zh2)
    k = V(vec.transpose(T.tab[:], T.zh2[:]))
    vw(k)
    k = tt(T.gm[:], T.tab[:].indirect(T.rho[:, 0:32]), T.mk[:], A.mult)
    vw(k)
    k = hold(T.gs[:], T.h16[:], T.gm[:])
    vw(k)
    k = tt(T.pf[:], T.gs[:, 15:512:16], T.bp[:], A.add)
    vw(k)
    k_po = copy(T.po16[:], T.pf[:])
    k = tt(T.pu[:], T.pf[:], T.eu[:], A.add)
    vw(k)
    copy(T.pu16[:], T.pu[:])

    wait("v", "xo", 32)
    wait("s", "xo", 32)
    wait("s", "vs", k_po)
    wait("v", "axc", ARR)
    wait("s", "axs", ARR)
    k_xk, s_xk = [], []
    for kk in range(2):
        o, w = S * kk, 16 * kk
        k_xk.append(copy(words(T.xk[:, o:o + S]), words(T.xp[:, 0:POOL]).indirect(T.po16[:, w:w + 16])))
        s_xk.append(act(T.xks[:, o:o + S], T.xps[:, 0:POOL].indirect(T.po16[:, w:w + 16])))
    ps = [T.ps0, T.ps1, T.ps2, T.ps3]
    t_p = [0] * 4
    for kk in range(2):
        wait("t", "vs", k_xk[kk])
        wait("t", "ss", s_xk[kk])
        o = S * kk
        for b in range(4):
            w = 128 * (4 * kk + b)
            t_p[b] = did("ts", ten.matmul_mx(ps[b][:, 0:S], T.aq[:, w:w + 128], T.aqs[:, w:w + 128],
                                             T.xk[:, o:o + S], T.xks[:, o:o + S], kk == 0, kk == 1))
    wait("v", "ru", 128)
    vw(k_xk[1])
    k_xu = copy(words(T.xu[:, 0:336]), words(T.xk[:, 0:2 * S]).indirect(T.lru[:, 0:21]))
    wait("s", "ru", 128)
    wait("s", "ss", s_xk[1])
    s_xu = act(T.xus[:, 0:336], T.xks[:, 0:2 * S].indirect(T.lru[:, 0:21]))
    wait("g", "vs", k_xu)
    send(lambda i: T.xu[:, 48 * i:48 * i + 48].bitcast(dt.uint8),
         lambda j: T.up[:, 512 + 48 * j:560 + 48 * j].bitcast(dt.uint8), "auc")
    wait("g", "ss", s_xu)
    send(lambda i: T.xus[:, 48 * i:48 * i + 48], lambda j: T.ups[:, 512 + 48 * j:560 + 48 * j], "aus")
    wait("y", "vs", k_xk[1])
    wait("y", "ss", s_xk[1])
    load("y", T.up[:, 0:512].bitcast(dt.uint8), T.xk[:].bitcast(dt.uint8), "uc")
    load("y", T.ups[:, 0:512], T.xks[:], "uc")
    for b in range(4):
        out = T.ht[:, b:4 * S:4]
        if b % 2 == 0:
            wait("s", "ts", t_p[b])
            s_r = act(out, ps[b][:, 0:S], Fn.Relu, scale=0.05)
        else:
            wait("v", "ts", t_p[b])
            k = ts(out, ps[b][:, 0:S], 0.0, A.max, 0.05, A.mult)
    wait("v", "ss", s_r)
    vw(k)
    k_hq = quant(T.hq[:], T.hqs[:], T.ht[:])
    vw(k_hq)
    k_hs = copy(words(T.hg[:, 0:224]), words(T.hq[:, 0:S]).indirect(T.lr[:, 0:14]))
    wait("s", "vs", k_hq)
    s_hs = act(T.hgs[:, 0:224], T.hqs[:, 0:S].indirect(T.lr[:, 0:14]))
    wait("g", "vs", k_hs)
    send(lambda i: T.hg[:, 32 * i:32 * i + C1].bitcast(dt.uint8),
         lambda j: T.hp[:, S + C1 * j:S + C1 * j + C1].bitcast(dt.uint8), "ahc")
    wait("g", "ss", s_hs)
    send(lambda i: T.hgs[:, 32 * i:32 * i + C1], lambda j: T.hps[:, S + C1 * j:S + C1 * j + C1], "ahs")
    k_hp = quant(T.hp[:, 0:S], T.hps[:, 0:S], T.ht[:])
    wait("v", "lv", 32)
    quant(T.vq[:], T.vqs[:], T.vb[:])
    quant(T.uq[:], T.uqs[:], T.ub[:])

    wait("v", "uc", 32)
    wait("v", "auc", ARR)
    k_yu = copy(words(T.yu[:]), words(T.up[:, 0:UPOOL]).indirect(T.pu16[:, 0:32]))
    wait("s", "vs", k_hp)
    wait("s", "uc", 32)
    wait("s", "aus", ARR)
    s_yu = act(T.yus[:], T.ups[:, 0:UPOOL].indirect(T.pu16[:, 0:32]))
    wait("t", "vs", k_yu)
    wait("t", "ss", s_yu)
    for kk in range(2):
        o, w = S * kk, 128 * kk
        did("ts", ten.matmul_mx(T.psy[:, 0:S], T.uq[:, w:w + 128], T.uqs[:, w:w + 128],
                                T.yu[:, o:o + S], T.yus[:, o:o + S], kk == 0, False))
    wait("v", "ahc", ARR)
    wait("s", "ahs", ARR)
    vw(k_hp)
    for kk in range(2):
        o, w = S * kk, 16 * kk
        k = copy(words(T.yh[:, o:o + S]), words(T.hp[:, 0:POOL]).indirect(T.po16[:, w:w + 16]))
        s = act(T.yhs[:, o:o + S], T.hps[:, 0:POOL].indirect(T.po16[:, w:w + 16]))
        wait("t", "vs", k)
        wait("t", "ss", s)
        w = 128 * kk
        t_y = did("ts", ten.matmul_mx(T.psy[:, 0:S], T.vq[:, w:w + 128], T.vqs[:, w:w + 128],
                                      T.yh[:, o:o + S], T.yhs[:, o:o + S], False, kk == 1))
    wait("v", "ts", t_y)
    k = copy(T.yo[:], T.psy[:, 0:S])
    wait("y", "vs", k)
    load("y", T.y[:], T.yo[:], "st")

    ends = {"lw": 128, "lw2": 256, "lx": 16, "la": 16, "lv": 32, "rt": 64, "rf": 128, "ru": 128, "xo": 32, "uc": 32,
            "ls": 8 * ARR, "af": ARR, "au": ARR, "axc": ARR, "axs": ARR, "auc": ARR, "aus": ARR, "ahc": ARR,
            "ahs": ARR, "st": 16, **cnt}
    for name in ends:
        wait("g", name, ends[name])
